import numpy as np
import ml_dtypes


def mxq(x, axis, fmt="e4m3"):
    dtype, down = {"e4m3": (ml_dtypes.float8_e4m3fn, 7), "e5m2": (ml_dtypes.float8_e5m2, 14)}[fmt]
    v = np.moveaxis(np.asarray(x, np.float32).astype(ml_dtypes.bfloat16).astype(np.float64), axis, -1)
    blocks = v.reshape(v.shape[:-1] + (-1, 32))
    amax = np.abs(blocks).max(-1, keepdims=True)
    byte = np.maximum(np.where(amax > 0, np.frexp(amax)[1] - 1 + 127, 0) - down, 1)
    scale = np.exp2(byte - 127.0)
    codes = (blocks / scale).astype(np.float32).astype(dtype).astype(np.float64)
    return np.moveaxis((codes * scale).reshape(v.shape), -1, axis)


WIDE = False


def mx_kscale(k):
    if not WIDE:
        return np.ones(k)
    levels = np.array([30, -30])
    if k % 512:
        return np.exp2(np.random.permutation(np.resize(levels, k // 32))).repeat(32)
    a = np.empty((k // 512, 16))
    for p in range(k // 512):
        a[p, :8] = np.random.permutation(np.resize(levels, 8))
        for g in range(8):
            far = levels[np.abs(levels - a[p, g]) >= 10]
            a[p, g + 8] = far[np.random.randint(len(far))]
    return np.exp2(a.ravel()).repeat(32)


def f64(x):
    return np.asarray(x).astype(np.float64)


E2M1 = np.array([0.0, 0.5, 1.0, 1.5, 2.0, 3.0, 4.0, 6.0, -0.0, -0.5, -1.0, -1.5, -2.0, -3.0, -4.0, -6.0])


def pack_weight(w, fmt):
    k, n = w.shape
    w = f64(np.asarray(w, np.float32).astype(ml_dtypes.bfloat16)).reshape(k // 32, 32, n)
    amax = np.abs(w).max(1)
    if fmt == "e4m3":
        byte = np.frexp(amax)[1] - 1 + 127 - 7
    else:
        mant, ex = np.frexp(amax / 6.0)
        byte = np.where(mant > 0.5, ex, ex - 1) + 127
    byte = np.clip(np.where(amax > 0, byte, 1), 1, 254)
    scaled = (w * np.exp2(127.0 - byte)[:, None, :]).reshape(k, n).astype(np.float32)
    by_word = np.ascontiguousarray(scaled.reshape(k // 512, 128, 4, n).transpose(0, 1, 3, 2))
    if fmt == "e4m3":
        words = by_word.astype(ml_dtypes.float8_e4m3fn).view(np.uint8)
    else:
        c = by_word.astype(ml_dtypes.float4_e2m1fn).view(np.uint8) & 0xF
        words = (c[..., 0::2] | (c[..., 1::2] << 4)).reshape(k // 512, 128, 2 * n)
    return np.ascontiguousarray(words), np.ascontiguousarray(byte.astype(np.uint8).reshape(k // 512, 16, n))


def unpack_weight(words, scales, fmt):
    g, _, n = scales.shape
    words = np.ascontiguousarray(words).reshape(g, 128, n, -1)
    if fmt == "e4m3":
        vals = words.view(ml_dtypes.float8_e4m3fn).astype(np.float64)
    else:
        nib = np.empty((g, 128, n, 4), np.uint8)
        nib[..., 0::2] = words & 0xF
        nib[..., 1::2] = words >> 4
        vals = E2M1[nib]
    vals = vals * np.repeat(np.exp2(scales.astype(np.float64) - 127.0), 8, axis=1)[..., None]
    return vals.transpose(0, 1, 3, 2).reshape(g * 512, n)


N, L, R, K, T = 512, 1024, 512, 512, 512


def setup_inputs():
    n = np.random.standard_normal
    fn = mx_kscale(N)
    fl = mx_kscale(L)
    fr = mx_kscale(R)
    wdp = pack_weight(n((N, R)) * 1 / np.sqrt(N) * fn[:, None], "e2m1")
    xqp = pack_weight(n((L, T)) / fl[:, None], "e4m3")
    wsp = pack_weight(n((L, R)) * 1 / np.sqrt(L) * fl[:, None], "e2m1")
    wup = pack_weight(n((R, K)) * 1 / np.sqrt(R) / fr[:, None], "e4m3")
    return {
        "g": (n((N, T)) * np.exp(0.5 * n((1, T))) / fn[:, None]).astype(np.float32),
        "wd_words": wdp[0],
        "wd_scales": wdp[1],
        "xq_words": xqp[0],
        "xq_scales": xqp[1],
        "ws_words": wsp[0],
        "ws_scales": wsp[1],
        "us": (np.random.uniform(0.5, 2.0, (R, 1)) * fr[:, None]).astype(np.float32),
        "wu_words": wup[0],
        "wu_scales": wup[1],
    }


def reference(g, wd_words, wd_scales, xq_words, xq_scales, ws_words, ws_scales, us, wu_words, wu_scales):
    wdu = unpack_weight(wd_words, wd_scales, "e2m1")
    xqu = unpack_weight(xq_words, xq_scales, "e4m3")
    wsu = unpack_weight(ws_words, ws_scales, "e2m1")
    wuu = unpack_weight(wu_words, wu_scales, "e4m3")
    gq = mxq(f64(g), 0, "e5m2")
    d = wdu.T @ gq + wsu.T @ xqu
    dc = np.maximum(np.minimum(d, 1.0), 0.0 - 1.0) * f64(us)
    dcq = mxq(dc, 0, "e5m2")
    y = wuu.T @ dcq
    return y

@@ -1,0 +1,247 @@
+from contextlib import ExitStack
+
+import concourse.mybir as mybir
+from concourse.masks import make_identity
+
+N, L, R, K, T = 512, 1024, 512, 512, 512
+FLOPS = 2 * T * (N * R + L * R + R * K)
+
+F32 = mybir.dt.float32
+BF16 = mybir.dt.bfloat16
+I32 = mybir.dt.int32
+U32 = mybir.dt.uint32
+U8 = mybir.dt.uint8
+E4M3 = mybir.dt.float8_e4m3fn_x4
+E5M2 = mybir.dt.float8_e5m2_x4
+E2M1 = mybir.dt.float4_e2m1fn_x4
+ALU = mybir.AluOpType
+ACT = mybir.ActivationFunctionType
+
+P = 128
+PACK = 4
+TC = 128
+CHUNKS = T // TC
+HALF = T // 2
+WARM_PASSES = 8
+WD, WS, XQ = 0, 1, 3
+
+
+def tile_mix_gradient_clipped_between_kernel(
+    tc, g, wd_words, wd_scales, xq_words, xq_scales, ws_words, ws_scales, us, wu_words, wu_scales, out
+):
+    nc = tc.nc
+    with ExitStack() as ctx:
+        sb = ctx.enter_context(tc.tile_pool(name="sb", bufs=1))
+        ps = ctx.enter_context(tc.psum_pool(name="ps", bufs=1))
+        ctx.enter_context(tc.manual_schedule())
+
+        g_raw = [sb.tile([P, PACK, w], F32, name="g_raw%d" % i) for i, w in enumerate((TC, TC, HALF))]
+        g_src = [g_raw[0][:], g_raw[1][:], g_raw[2][:, :, 0:TC], g_raw[2][:, :, TC:HALF]]
+        g_bf = [sb.tile([P, TC * PACK], BF16, name="g_bf%d" % c, align_bytes=64) for c in range(CHUNKS)]
+        g_codes = [sb.tile([P, TC], U32, name="g_codes%d" % c, align_bytes=64) for c in range(CHUNKS)]
+        g_plane = [sb.tile([P, TC], U8, name="g_plane%d" % c, align_bytes=64) for c in range(CHUNKS)]
+        xq = [sb.tile([P, 2, HALF], U32, name="xq%d" % h, align_bytes=64) for h in range(2)]
+        wd = sb.tile([P, 2 * R], U8, align_bytes=64)
+        ws = sb.tile([P, 2, 2 * R], U8, align_bytes=64)
+        wu = sb.tile([P, K], U32, align_bytes=64)
+        planes = sb.tile([P, 5 * 512], U8, align_bytes=64)
+        staged = sb.tile([16, 5 * 128], I32, align_bytes=64)
+        act_warm = sb.tile([P, 2], BF16)
+        wu_plane = sb.tile([P, 1, K], U8, align_bytes=64)
+        zero_bf = sb.tile([P, TC * PACK], BF16, align_bytes=64)
+        zero_codes = sb.tile([P, TC], U32, align_bytes=64)
+        zero_plane = sb.tile([P, TC], U8, align_bytes=64)
+        u_cols = sb.tile([P, PACK], F32)
+        ident = sb.tile([P, P], F32)
+        clipped = [sb.tile([P, PACK, P], F32, name="clipped%d" % c) for c in range(CHUNKS)]
+        dc_bf = [sb.tile([P, TC * PACK], BF16, name="dc_bf%d" % c, align_bytes=64) for c in range(CHUNKS)]
+        dc_codes = sb.tile([P, T + T], U32, align_bytes=64)
+        dc_plane = sb.tile([P, T + T], U8, align_bytes=64)
+        res = [[sb.tile([P, HALF], F32, name="res%d_%d" % (h, m)) for m in range(4)] for h in range(2)]
+
+        g_view = g.rearrange("(p j) t -> p j t", j=PACK)
+        xq_view = xq_words.rearrange("z p c r -> p z (c r)").bitcast(I32)
+
+        def load_scales(eng, plane, src, q):
+            eng.dma_start(
+                out=plane[32 * q : 32 * q + 4, :, :].bitcast(I32),
+                in_=src.bitcast(I32).rearrange("z s c -> s z c")[4 * q : 4 * q + 4, :, :],
+            )
+
+        def zero(eng, ap):
+            eng.memset(ap.bitcast(I32), 0)
+
+        def stage_scales(eng, src, first):
+            z = src.shape[0]
+            eng.dma_start(
+                out=staged[:, first * 128 : (first + z) * 128].rearrange("s (z c) -> s z c", z=z),
+                in_=src.bitcast(I32).rearrange("z s c -> s z c"),
+            )
+
+        planes_w = planes[:].bitcast(I32)
+        nc.gpsimd.memset(zero_bf[:], 0.0)
+        zero(nc.gpsimd, planes[:])
+        zero(nc.vector, dc_codes[:, TC:T])
+        zero(nc.vector, dc_plane[:, TC:T])
+        nc.vector.quantize_mx(out=zero_codes[:].bitcast(E4M3), scales=zero_plane[:], in_=zero_bf[:])
+        nc.vector.quantize_mx(out=dc_codes[:, 0:TC].bitcast(E5M2), scales=dc_plane[:, 0:TC], in_=zero_bf[:])
+        zero(nc.vector, wu_plane[:])
+
+        stage_scales(nc.sync, wd_scales, WD)
+        stage_scales(nc.scalar, ws_scales, WS)
+        stage_scales(nc.scalar, xq_scales, XQ)
+        nc.sync.dma_start(out=g_raw[0][:], in_=g_view[:, :, 0:TC])
+        nc.sync.dma_start(out=xq[0][:].bitcast(I32), in_=xq_view[:, :, 0:HALF])
+        nc.sync.dma_start(out=ws[:].bitcast(I32), in_=ws_words.rearrange("z p c -> p z c").bitcast(I32))
+        nc.sync.dma_start(out=wd[:].bitcast(I32), in_=wd_words[0].bitcast(I32))
+        nc.sync.dma_start(out=g_raw[1][:], in_=g_view[:, :, TC:HALF])
+        nc.scalar.copy(out=act_warm[:], in_=zero_bf[:, 0:2])
+        for q in range(1, 4):
+            nc.scalar.dma_start(out=planes_w[32 * q : 32 * q + 4, :], in_=staged[4 * q : 4 * q + 4, :])
+        nc.vector.tensor_copy(out=planes_w[0:4, :], in_=staged[0:4, :])
+        nc.sync.dma_start(out=g_raw[2][:], in_=g_view[:, :, HALF:T])
+        nc.sync.dma_start(out=xq[1][:].bitcast(I32), in_=xq_view[:, :, HALF:T])
+        nc.sync.dma_start(out=u_cols[:], in_=us.rearrange("(p j) o -> p (j o)", j=PACK))
+        nc.sync.dma_start(out=wu[:].bitcast(I32), in_=wu_words[0].rearrange("p c r -> p (c r)").bitcast(I32))
+        for q in range(4):
+            load_scales(nc.sync, wu_plane, wu_scales, q)
+        make_identity(nc, ident[:])
+
+        warm = ps.tile([P, T], F32, name="y_bank", tag="early0")
+        for i in range(WARM_PASSES):
+            nc.tensor.matmul_mx(
+                out=warm[:],
+                lhsT=zero_codes[:].bitcast(E4M3),
+                lhsT_scale=zero_plane[:],
+                rhs=dc_codes[:, 0:T].bitcast(E5M2),
+                rhs_scale=dc_plane[:, 0:T],
+                start=True,
+                stop=True,
+            )
+
+        d_bank = [ps.tile([P, R], F32, name="d_bank%d" % c) for c in range(CHUNKS)]
+
+        def interleave_g(c):
+            nc.scalar.copy(
+                out=g_bf[c][:].rearrange("p (c i j) -> p c j i", i=4, j=PACK),
+                in_=g_src[c].rearrange("p j (c i) -> p c j i", i=4),
+            )
+
+        def quantize_g(c):
+            nc.vector.quantize_mx(out=g_codes[c][:].bitcast(E5M2), scales=g_plane[c][:], in_=g_bf[c][:])
+
+        def x_pass(c, z):
+            lo = (c % 2) * TC
+            nc.tensor.matmul_mx(
+                out=d_bank[c][:],
+                lhsT=xq[c // 2][:, z, lo : lo + TC].bitcast(E4M3),
+                lhsT_scale=planes[:, (XQ + z) * 512 + c * TC : (XQ + z) * 512 + (c + 1) * TC],
+                rhs=ws[:, z, :].bitcast(E2M1),
+                rhs_scale=planes[:, (WS + z) * 512 : (WS + z + 1) * 512],
+                start=(z == 0),
+                stop=False,
+            )
+
+        def g_pass(c):
+            nc.tensor.matmul_mx(
+                out=d_bank[c][:],
+                lhsT=g_codes[c][:].bitcast(E5M2),
+                lhsT_scale=g_plane[c][:],
+                rhs=wd[:].bitcast(E2M1),
+                rhs_scale=planes[:, WD * 512 : (WD + 1) * 512],
+                start=False,
+                stop=True,
+            )
+
+        def clip(c):
+            nc.vector.tensor_scalar(
+                out=clipped[c][:],
+                in0=d_bank[c][:].rearrange("t (p j) -> t j p", j=PACK),
+                scalar1=1.0,
+                scalar2=-1.0,
+                op0=ALU.min,
+                op1=ALU.max,
+            )
+
+        turned = {}
+
+        def turn(c):
+            bank = ps.tile([P, PACK, TC], F32, name="turned", tag="turned%d" % (c % 2))
+            turned[c] = bank
+            for j in range(PACK):
+                nc.tensor.transpose(bank[:, j, :], clipped[c][:, j, :], ident[:])
+
+        def scale(c):
+            nc.vector.tensor_tensor(
+                out=dc_bf[c][:].rearrange("p (t j) -> p t j", j=PACK),
+                in0=turned[c][:].rearrange("p j t -> p t j"),
+                in1=u_cols[:].unsqueeze(1).to_broadcast([P, TC, PACK]),
+                op=ALU.mult,
+            )
+
+        def quantize_dc(c):
+            cols = slice(T + c * TC, T + (c + 1) * TC)
+            nc.vector.quantize_mx(out=dc_codes[:, cols].bitcast(E5M2), scales=dc_plane[:, cols], in_=dc_bf[c][:])
+
+        y_bank = {}
+
+        def y_pass(h, m, tag):
+            bank = ps.tile([P, T], F32, name="y_bank", tag=tag)
+            y_bank[h, m] = bank
+            cols = slice((h + 1) * HALF, (h + 1) * HALF + T)
+            nc.tensor.matmul_mx(
+                out=bank[:],
+                lhsT=wu[:, m * P : (m + 1) * P].bitcast(E4M3),
+                lhsT_scale=wu_plane[:, 0, m * P : (m + 1) * P],
+                rhs=dc_codes[:, cols].bitcast(E5M2),
+                rhs_scale=dc_plane[:, cols],
+                start=True,
+                stop=True,
+            )
+
+        def y_out(h, m, on_vector):
+            if on_vector:
+                nc.vector.tensor_copy(out=res[h][m][:], in_=y_bank[h, m][:, HALF:T])
+            else:
+                nc.scalar.copy(out=res[h][m][:], in_=y_bank[h, m][:, HALF:T])
+            nc.sync.dma_start(out=out[m * P : (m + 1) * P, h * HALF : (h + 1) * HALF], in_=res[h][m][:])
+
+        for c in range(CHUNKS):
+            interleave_g(c)
+        quantize_g(0)
+        quantize_g(1)
+        for c in range(2):
+            x_pass(c, 0)
+            x_pass(c, 1)
+            g_pass(c)
+        clip(0)
+        quantize_g(2)
+        clip(1)
+        quantize_g(3)
+        turn(0)
+        x_pass(2, 0)
+        x_pass(2, 1)
+        g_pass(2)
+        turn(1)
+        x_pass(3, 0)
+        x_pass(3, 1)
+        g_pass(3)
+        scale(0)
+        clip(2)
+        turn(2)
+        scale(1)
+        clip(3)
+        turn(3)
+        quantize_dc(0)
+        quantize_dc(1)
+        scale(2)
+        for m, tag in enumerate(("early0", "early1", "d_bank0", "d_bank1")):
+            y_pass(0, m, tag)
+            y_out(0, m, False)
+        scale(3)
+        quantize_dc(2)
+        quantize_dc(3)
+        for m, tag in enumerate(("d_bank2", "d_bank3", "turned0", "turned1")):
+            y_pass(1, m, tag)
+        for m in range(4):
+            y_out(1, m, m % 2 == 0)

@@ -22,7 +22,7 @@ PACK = 4
 TC = 128
 CHUNKS = T // TC
 HALF = T // 2
-WARM_PASSES = 8
+WARM_PASSES = 9
 WD, WS, XQ = 0, 1, 3
 
 
@@ -35,8 +35,8 @@ def tile_mix_gradient_clipped_between_kernel(
         ps = ctx.enter_context(tc.psum_pool(name="ps", bufs=1))
         ctx.enter_context(tc.manual_schedule())
 
-        g_raw = [sb.tile([P, PACK, w], F32, name="g_raw%d" % i) for i, w in enumerate((TC, TC, HALF))]
-        g_src = [g_raw[0][:], g_raw[1][:], g_raw[2][:, :, 0:TC], g_raw[2][:, :, TC:HALF]]
+        g_raw = [sb.tile([P, PACK, HALF], F32, name="g_raw%d" % h) for h in range(2)]
+        g_src = [g_raw[c // 2][:, :, (c % 2) * TC : (c % 2 + 1) * TC] for c in range(CHUNKS)]
         g_bf = [sb.tile([P, TC * PACK], BF16, name="g_bf%d" % c, align_bytes=64) for c in range(CHUNKS)]
         g_codes = [sb.tile([P, TC], U32, name="g_codes%d" % c, align_bytes=64) for c in range(CHUNKS)]
         g_plane = [sb.tile([P, TC], U8, name="g_plane%d" % c, align_bytes=64) for c in range(CHUNKS)]
@@ -79,36 +79,36 @@ def tile_mix_gradient_clipped_between_kernel(
             )
 
         planes_w = planes[:].bitcast(I32)
-        nc.gpsimd.memset(zero_bf[:], 0.0)
-        zero(nc.gpsimd, planes[:])
+        zero(nc.vector, zero_bf[:])
         zero(nc.vector, dc_codes[:, TC:T])
         zero(nc.vector, dc_plane[:, TC:T])
         nc.vector.quantize_mx(out=zero_codes[:].bitcast(E4M3), scales=zero_plane[:], in_=zero_bf[:])
         nc.vector.quantize_mx(out=dc_codes[:, 0:TC].bitcast(E5M2), scales=dc_plane[:, 0:TC], in_=zero_bf[:])
+        zero(nc.vector, planes[:])
         zero(nc.vector, wu_plane[:])
+        make_identity(nc, ident[:])
 
         stage_scales(nc.sync, wd_scales, WD)
         stage_scales(nc.scalar, ws_scales, WS)
         stage_scales(nc.scalar, xq_scales, XQ)
-        nc.sync.dma_start(out=g_raw[0][:], in_=g_view[:, :, 0:TC])
-        nc.sync.dma_start(out=xq[0][:].bitcast(I32), in_=xq_view[:, :, 0:HALF])
+        nc.scalar.copy(out=act_warm[:], in_=zero_bf[:, 0:2])
+        nc.sync.dma_start(out=g_raw[0][:], in_=g_view[:, :, 0:HALF])
         nc.sync.dma_start(out=ws[:].bitcast(I32), in_=ws_words.rearrange("z p c -> p z c").bitcast(I32))
         nc.sync.dma_start(out=wd[:].bitcast(I32), in_=wd_words[0].bitcast(I32))
-        nc.sync.dma_start(out=g_raw[1][:], in_=g_view[:, :, TC:HALF])
-        nc.scalar.copy(out=act_warm[:], in_=zero_bf[:, 0:2])
         for q in range(1, 4):
-            nc.scalar.dma_start(out=planes_w[32 * q : 32 * q + 4, :], in_=staged[4 * q : 4 * q + 4, :])
+            nc.sync.dma_start(out=planes_w[32 * q : 32 * q + 4, :], in_=staged[4 * q : 4 * q + 4, :])
         nc.vector.tensor_copy(out=planes_w[0:4, :], in_=staged[0:4, :])
-        nc.sync.dma_start(out=g_raw[2][:], in_=g_view[:, :, HALF:T])
+        nc.sync.dma_start(out=xq[0][:].bitcast(I32), in_=xq_view[:, :, 0:HALF])
+        nc.sync.dma_start(out=g_raw[1][:], in_=g_view[:, :, HALF:T])
         nc.sync.dma_start(out=xq[1][:].bitcast(I32), in_=xq_view[:, :, HALF:T])
         nc.sync.dma_start(out=u_cols[:], in_=us.rearrange("(p j) o -> p (j o)", j=PACK))
         nc.sync.dma_start(out=wu[:].bitcast(I32), in_=wu_words[0].rearrange("p c r -> p (c r)").bitcast(I32))
         for q in range(4):
             load_scales(nc.sync, wu_plane, wu_scales, q)
-        make_identity(nc, ident[:])
 
         warm = ps.tile([P, T], F32, name="y_bank", tag="early0")
-        for i in range(WARM_PASSES):
+
+        def warm_pass():
             nc.tensor.matmul_mx(
                 out=warm[:],
                 lhsT=zero_codes[:].bitcast(E4M3),
@@ -118,6 +118,9 @@ def tile_mix_gradient_clipped_between_kernel(
                 start=True,
                 stop=True,
             )
+
+        for i in range(WARM_PASSES):
+            warm_pass()
 
         d_bank = [ps.tile([P, R], F32, name="d_bank%d" % c) for c in range(CHUNKS)]
 
@@ -165,8 +168,8 @@ def tile_mix_gradient_clipped_between_kernel(
 
         turned = {}
 
-        def turn(c):
-            bank = ps.tile([P, PACK, TC], F32, name="turned", tag="turned%d" % (c % 2))
+        def turn(c, tag):
+            bank = ps.tile([P, PACK, TC], F32, name="turned", tag=tag)
             turned[c] = bank
             for j in range(PACK):
                 nc.tensor.transpose(bank[:, j, :], clipped[c][:, j, :], ident[:])
@@ -218,20 +221,21 @@ def tile_mix_gradient_clipped_between_kernel(
         quantize_g(2)
         clip(1)
         quantize_g(3)
-        turn(0)
+        turn(0, "turned0")
         x_pass(2, 0)
         x_pass(2, 1)
         g_pass(2)
-        turn(1)
+        turn(1, "turned1")
         x_pass(3, 0)
         x_pass(3, 1)
         g_pass(3)
         scale(0)
         clip(2)
-        turn(2)
+        turn(2, "turned0")
+        warm_pass()
         scale(1)
         clip(3)
-        turn(3)
+        turn(3, "turned1")
         quantize_dc(0)
         quantize_dc(1)
         scale(2)

@@ -22,7 +22,7 @@ PACK = 4
 TC = 128
 CHUNKS = T // TC
 HALF = T // 2
-WARM_PASSES = 9
+WARM_PASSES = 8
 WD, WS, XQ = 0, 1, 3
 
 
@@ -79,29 +79,29 @@ def tile_mix_gradient_clipped_between_kernel(
             )
 
         planes_w = planes[:].bitcast(I32)
+        zero(nc.gpsimd, planes[:])
+        zero(nc.gpsimd, wu_plane[:])
+        make_identity(nc, ident[:])
         zero(nc.vector, zero_bf[:])
         zero(nc.vector, dc_codes[:, TC:T])
         zero(nc.vector, dc_plane[:, TC:T])
         nc.vector.quantize_mx(out=zero_codes[:].bitcast(E4M3), scales=zero_plane[:], in_=zero_bf[:])
         nc.vector.quantize_mx(out=dc_codes[:, 0:TC].bitcast(E5M2), scales=dc_plane[:, 0:TC], in_=zero_bf[:])
-        zero(nc.vector, planes[:])
-        zero(nc.vector, wu_plane[:])
-        make_identity(nc, ident[:])
 
         stage_scales(nc.sync, wd_scales, WD)
-        stage_scales(nc.scalar, ws_scales, WS)
         stage_scales(nc.scalar, xq_scales, XQ)
+        stage_scales(nc.sync, ws_scales, WS)
+        nc.scalar.dma_start(out=u_cols[:], in_=us.rearrange("(p j) o -> p (j o)", j=PACK))
         nc.scalar.copy(out=act_warm[:], in_=zero_bf[:, 0:2])
         nc.sync.dma_start(out=g_raw[0][:], in_=g_view[:, :, 0:HALF])
         nc.sync.dma_start(out=ws[:].bitcast(I32), in_=ws_words.rearrange("z p c -> p z c").bitcast(I32))
-        nc.sync.dma_start(out=wd[:].bitcast(I32), in_=wd_words[0].bitcast(I32))
+        nc.sync.dma_start(out=xq[0][:].bitcast(I32), in_=xq_view[:, :, 0:HALF])
         for q in range(1, 4):
             nc.sync.dma_start(out=planes_w[32 * q : 32 * q + 4, :], in_=staged[4 * q : 4 * q + 4, :])
         nc.vector.tensor_copy(out=planes_w[0:4, :], in_=staged[0:4, :])
-        nc.sync.dma_start(out=xq[0][:].bitcast(I32), in_=xq_view[:, :, 0:HALF])
+        nc.sync.dma_start(out=wd[:].bitcast(I32), in_=wd_words[0].bitcast(I32))
         nc.sync.dma_start(out=g_raw[1][:], in_=g_view[:, :, HALF:T])
         nc.sync.dma_start(out=xq[1][:].bitcast(I32), in_=xq_view[:, :, HALF:T])
-        nc.sync.dma_start(out=u_cols[:], in_=us.rearrange("(p j) o -> p (j o)", j=PACK))
         nc.sync.dma_start(out=wu[:].bitcast(I32), in_=wu_words[0].rearrange("p c r -> p (c r)").bitcast(I32))
         for q in range(4):
             load_scales(nc.sync, wu_plane, wu_scales, q)
@@ -157,14 +157,15 @@ def tile_mix_gradient_clipped_between_kernel(
             )
 
         def clip(c):
-            nc.vector.tensor_scalar(
-                out=clipped[c][:],
-                in0=d_bank[c][:].rearrange("t (p j) -> t j p", j=PACK),
-                scalar1=1.0,
-                scalar2=-1.0,
-                op0=ALU.min,
-                op1=ALU.max,
-            )
+            for j in (0, 2):
+                nc.vector.tensor_scalar(
+                    out=clipped[c][:, j : j + 2, :],
+                    in0=d_bank[c][:].rearrange("t (p j) -> t j p", j=PACK)[:, j : j + 2, :],
+                    scalar1=1.0,
+                    scalar2=-1.0,
+                    op0=ALU.min,
+                    op1=ALU.max,
+                )
 
         turned = {}
 
@@ -218,8 +219,8 @@ def tile_mix_gradient_clipped_between_kernel(
             x_pass(c, 1)
             g_pass(c)
         clip(0)
-        quantize_g(2)
         clip(1)
+        quantize_g(2)
         quantize_g(3)
         turn(0, "turned0")
         x_pass(2, 0)

@@ -22,7 +22,7 @@ PACK = 4
 TC = 128
 CHUNKS = T // TC
 HALF = T // 2
-WARM_PASSES = 8
+WARM_PASSES = 9
 WD, WS, XQ = 0, 1, 3
 
 
@@ -35,8 +35,8 @@ def tile_mix_gradient_clipped_between_kernel(
         ps = ctx.enter_context(tc.psum_pool(name="ps", bufs=1))
         ctx.enter_context(tc.manual_schedule())
 
-        g_raw = [sb.tile([P, PACK, HALF], F32, name="g_raw%d" % h) for h in range(2)]
-        g_src = [g_raw[c // 2][:, :, (c % 2) * TC : (c % 2 + 1) * TC] for c in range(CHUNKS)]
+        g_raw = sb.tile([P, PACK, T], F32)
+        g_src = [g_raw[:, :, c * TC : (c + 1) * TC] for c in range(CHUNKS)]
         g_bf = [sb.tile([P, TC * PACK], BF16, name="g_bf%d" % c, align_bytes=64) for c in range(CHUNKS)]
         g_codes = [sb.tile([P, TC], U32, name="g_codes%d" % c, align_bytes=64) for c in range(CHUNKS)]
         g_plane = [sb.tile([P, TC], U8, name="g_plane%d" % c, align_bytes=64) for c in range(CHUNKS)]
@@ -45,7 +45,7 @@ def tile_mix_gradient_clipped_between_kernel(
         ws = sb.tile([P, 2, 2 * R], U8, align_bytes=64)
         wu = sb.tile([P, K], U32, align_bytes=64)
         planes = sb.tile([P, 5 * 512], U8, align_bytes=64)
-        staged = sb.tile([16, 5 * 128], I32, align_bytes=64)
+        staged = sb.tile([P, 5 * 128], I32, align_bytes=64)
         act_warm = sb.tile([P, 2], BF16)
         wu_plane = sb.tile([P, 1, K], U8, align_bytes=64)
         zero_bf = sb.tile([P, TC * PACK], BF16, align_bytes=64)
@@ -71,11 +71,11 @@ def tile_mix_gradient_clipped_between_kernel(
         def zero(eng, ap):
             eng.memset(ap.bitcast(I32), 0)
 
-        def stage_scales(eng, src, first):
+        def stage_scales(eng, src, first, h):
             z = src.shape[0]
             eng.dma_start(
-                out=staged[:, first * 128 : (first + z) * 128].rearrange("s (z c) -> s z c", z=z),
-                in_=src.bitcast(I32).rearrange("z s c -> s z c"),
+                out=staged[64 * h : 64 * h + 8, first * 128 : (first + z) * 128].rearrange("s (z c) -> s z c", z=z),
+                in_=src.bitcast(I32).rearrange("z s c -> s z c")[8 * h : 8 * h + 8, :, :],
             )
 
         planes_w = planes[:].bitcast(I32)
@@ -88,20 +88,21 @@ def tile_mix_gradient_clipped_between_kernel(
         nc.vector.quantize_mx(out=zero_codes[:].bitcast(E4M3), scales=zero_plane[:], in_=zero_bf[:])
         nc.vector.quantize_mx(out=dc_codes[:, 0:TC].bitcast(E5M2), scales=dc_plane[:, 0:TC], in_=zero_bf[:])
 
-        stage_scales(nc.sync, wd_scales, WD)
-        stage_scales(nc.scalar, xq_scales, XQ)
-        stage_scales(nc.sync, ws_scales, WS)
-        nc.scalar.dma_start(out=u_cols[:], in_=us.rearrange("(p j) o -> p (j o)", j=PACK))
+        for h, eng in enumerate((nc.sync, nc.scalar)):
+            stage_scales(eng, ws_scales, WS, h)
+            stage_scales(eng, xq_scales, XQ, h)
+            stage_scales(eng, wd_scales, WD, h)
         nc.scalar.copy(out=act_warm[:], in_=zero_bf[:, 0:2])
-        nc.sync.dma_start(out=g_raw[0][:], in_=g_view[:, :, 0:HALF])
+        nc.sync.dma_start(out=g_raw[:], in_=g_view)
+        nc.sync.dma_start(out=wd[:].bitcast(I32), in_=wd_words[0].bitcast(I32))
+        for h in range(2):
+            lo = 64 * h
+            nc.sync.dma_start(out=planes_w[lo + 32 : lo + 36, :], in_=staged[lo + 4 : lo + 8, :])
+            nc.vector.tensor_copy(out=planes_w[lo : lo + 4, :], in_=staged[lo : lo + 4, :])
         nc.sync.dma_start(out=ws[:].bitcast(I32), in_=ws_words.rearrange("z p c -> p z c").bitcast(I32))
         nc.sync.dma_start(out=xq[0][:].bitcast(I32), in_=xq_view[:, :, 0:HALF])
-        for q in range(1, 4):
-            nc.sync.dma_start(out=planes_w[32 * q : 32 * q + 4, :], in_=staged[4 * q : 4 * q + 4, :])
-        nc.vector.tensor_copy(out=planes_w[0:4, :], in_=staged[0:4, :])
-        nc.sync.dma_start(out=wd[:].bitcast(I32), in_=wd_words[0].bitcast(I32))
-        nc.sync.dma_start(out=g_raw[1][:], in_=g_view[:, :, HALF:T])
         nc.sync.dma_start(out=xq[1][:].bitcast(I32), in_=xq_view[:, :, HALF:T])
+        nc.sync.dma_start(out=u_cols[:], in_=us.rearrange("(p j) o -> p (j o)", j=PACK))
         nc.sync.dma_start(out=wu[:].bitcast(I32), in_=wu_words[0].rearrange("p c r -> p (c r)").bitcast(I32))
         for q in range(4):
             load_scales(nc.sync, wu_plane, wu_scales, q)
@@ -125,7 +126,8 @@ def tile_mix_gradient_clipped_between_kernel(
         d_bank = [ps.tile([P, R], F32, name="d_bank%d" % c) for c in range(CHUNKS)]
 
         def interleave_g(c):
-            nc.scalar.copy(
+            copy = nc.vector.tensor_copy if c < 2 else nc.scalar.copy
+            copy(
                 out=g_bf[c][:].rearrange("p (c i j) -> p c j i", i=4, j=PACK),
                 in_=g_src[c].rearrange("p j (c i) -> p c j i", i=4),
             )
@@ -141,8 +143,8 @@ def tile_mix_gradient_clipped_between_kernel(
                 lhsT_scale=planes[:, (XQ + z) * 512 + c * TC : (XQ + z) * 512 + (c + 1) * TC],
                 rhs=ws[:, z, :].bitcast(E2M1),
                 rhs_scale=planes[:, (WS + z) * 512 : (WS + z + 1) * 512],
-                start=(z == 0),
-                stop=False,
+                start=False,
+                stop=(z == 1),
             )
 
         def g_pass(c):
@@ -152,8 +154,8 @@ def tile_mix_gradient_clipped_between_kernel(
                 lhsT_scale=g_plane[c][:],
                 rhs=wd[:].bitcast(E2M1),
                 rhs_scale=planes[:, WD * 512 : (WD + 1) * 512],
-                start=False,
-                stop=True,
+                start=True,
+                stop=False,
             )
 
         def clip(c):
@@ -212,41 +214,35 @@ def tile_mix_gradient_clipped_between_kernel(
 
         for c in range(CHUNKS):
             interleave_g(c)
-        quantize_g(0)
-        quantize_g(1)
-        for c in range(2):
+        for c in range(CHUNKS):
+            quantize_g(c)
+        for c in range(3):
+            g_pass(c)
+        for c in range(3):
             x_pass(c, 0)
             x_pass(c, 1)
-            g_pass(c)
-        clip(0)
-        clip(1)
-        quantize_g(2)
-        quantize_g(3)
+            clip(c)
         turn(0, "turned0")
-        x_pass(2, 0)
-        x_pass(2, 1)
-        g_pass(2)
         turn(1, "turned1")
+        g_pass(3)
         x_pass(3, 0)
         x_pass(3, 1)
-        g_pass(3)
-        scale(0)
-        clip(2)
-        turn(2, "turned0")
+        turn(2, "d_bank0")
         warm_pass()
+        scale(0)
         scale(1)
         clip(3)
-        turn(3, "turned1")
+        turn(3, "d_bank1")
         quantize_dc(0)
         quantize_dc(1)
-        scale(2)
-        for m, tag in enumerate(("early0", "early1", "d_bank0", "d_bank1")):
+        for m, tag in enumerate(("early0", "early1", "turned0", "turned1")):
             y_pass(0, m, tag)
             y_out(0, m, False)
+        scale(2)
         scale(3)
         quantize_dc(2)
         quantize_dc(3)
-        for m, tag in enumerate(("d_bank2", "d_bank3", "turned0", "turned1")):
+        for m, tag in enumerate(("d_bank2", "d_bank3", "d_bank0", "d_bank1")):
             y_pass(1, m, tag)
         for m in range(4):
             y_out(1, m, m % 2 == 0)

from contextlib import ExitStack

import concourse.mybir as mybir
from concourse.masks import make_identity

N, L, R, K, T = 512, 1024, 512, 512, 512
FLOPS = 2 * T * (N * R + L * R + R * K)

F32 = mybir.dt.float32
BF16 = mybir.dt.bfloat16
I32 = mybir.dt.int32
U32 = mybir.dt.uint32
U8 = mybir.dt.uint8
E4M3 = mybir.dt.float8_e4m3fn_x4
E5M2 = mybir.dt.float8_e5m2_x4
E2M1 = mybir.dt.float4_e2m1fn_x4
ALU = mybir.AluOpType
ACT = mybir.ActivationFunctionType

P = 128
PACK = 4
TC = 128
CHUNKS = T // TC
HALF = T // 2
WARM_PASSES = 9
WD, WS, XQ = 0, 1, 3


def tile_mix_gradient_clipped_between_kernel(
    tc, g, wd_words, wd_scales, xq_words, xq_scales, ws_words, ws_scales, us, wu_words, wu_scales, out
):
    nc = tc.nc
    with ExitStack() as ctx:
        sb = ctx.enter_context(tc.tile_pool(name="sb", bufs=1))
        ps = ctx.enter_context(tc.psum_pool(name="ps", bufs=1))
        ctx.enter_context(tc.manual_schedule())

        g_raw = sb.tile([P, PACK, T], F32)
        g_src = [g_raw[:, :, c * TC : (c + 1) * TC] for c in range(CHUNKS)]
        g_bf = [sb.tile([P, TC * PACK], BF16, name="g_bf%d" % c, align_bytes=64) for c in range(CHUNKS)]
        g_codes = [sb.tile([P, TC], U32, name="g_codes%d" % c, align_bytes=64) for c in range(CHUNKS)]
        g_plane = [sb.tile([P, TC], U8, name="g_plane%d" % c, align_bytes=64) for c in range(CHUNKS)]
        xq = [sb.tile([P, 2, HALF], U32, name="xq%d" % h, align_bytes=64) for h in range(2)]
        wd = sb.tile([P, 2 * R], U8, align_bytes=64)
        ws = sb.tile([P, 2, 2 * R], U8, align_bytes=64)
        wu = sb.tile([P, K], U32, align_bytes=64)
        planes = sb.tile([P, 5 * 512], U8, align_bytes=64)
        staged = sb.tile([P, 5 * 128], I32, align_bytes=64)
        act_warm = sb.tile([P, 2], BF16)
        wu_plane = sb.tile([P, 1, K], U8, align_bytes=64)
        zero_bf = sb.tile([P, TC * PACK], BF16, align_bytes=64)
        zero_codes = sb.tile([P, TC], U32, align_bytes=64)
        zero_plane = sb.tile([P, TC], U8, align_bytes=64)
        u_cols = sb.tile([P, PACK], F32)
        ident = sb.tile([P, P], F32)
        clipped = [sb.tile([P, PACK, P], F32, name="clipped%d" % c) for c in range(CHUNKS)]
        dc_bf = [sb.tile([P, TC * PACK], BF16, name="dc_bf%d" % c, align_bytes=64) for c in range(CHUNKS)]
        dc_codes = sb.tile([P, T + T], U32, align_bytes=64)
        dc_plane = sb.tile([P, T + T], U8, align_bytes=64)
        res = [[sb.tile([P, HALF], F32, name="res%d_%d" % (h, m)) for m in range(4)] for h in range(2)]

        g_view = g.rearrange("(p j) t -> p j t", j=PACK)
        xq_view = xq_words.rearrange("z p c r -> p z (c r)").bitcast(I32)

        def load_scales(eng, plane, src, q):
            eng.dma_start(
                out=plane[32 * q : 32 * q + 4, :, :].bitcast(I32),
                in_=src.bitcast(I32).rearrange("z s c -> s z c")[4 * q : 4 * q + 4, :, :],
            )

        def zero(eng, ap):
            eng.memset(ap.bitcast(I32), 0)

        def stage_scales(eng, src, first, h):
            z = src.shape[0]
            eng.dma_start(
                out=staged[64 * h : 64 * h + 8, first * 128 : (first + z) * 128].rearrange("s (z c) -> s z c", z=z),
                in_=src.bitcast(I32).rearrange("z s c -> s z c")[8 * h : 8 * h + 8, :, :],
            )

        planes_w = planes[:].bitcast(I32)
        zero(nc.gpsimd, planes[:])
        zero(nc.gpsimd, wu_plane[:])
        make_identity(nc, ident[:])
        zero(nc.vector, zero_bf[:])
        zero(nc.vector, dc_codes[:, TC:T])
        zero(nc.vector, dc_plane[:, TC:T])
        nc.vector.quantize_mx(out=zero_codes[:].bitcast(E4M3), scales=zero_plane[:], in_=zero_bf[:])
        nc.vector.quantize_mx(out=dc_codes[:, 0:TC].bitcast(E5M2), scales=dc_plane[:, 0:TC], in_=zero_bf[:])

        for h, eng in enumerate((nc.sync, nc.scalar)):
            stage_scales(eng, ws_scales, WS, h)
            stage_scales(eng, xq_scales, XQ, h)
            stage_scales(eng, wd_scales, WD, h)
        nc.scalar.copy(out=act_warm[:], in_=zero_bf[:, 0:2])
        nc.sync.dma_start(out=g_raw[:], in_=g_view)
        nc.sync.dma_start(out=wd[:].bitcast(I32), in_=wd_words[0].bitcast(I32))
        for h in range(2):
            lo = 64 * h
            nc.sync.dma_start(out=planes_w[lo + 32 : lo + 36, :], in_=staged[lo + 4 : lo + 8, :])
            nc.vector.tensor_copy(out=planes_w[lo : lo + 4, :], in_=staged[lo : lo + 4, :])
        nc.sync.dma_start(out=ws[:].bitcast(I32), in_=ws_words.rearrange("z p c -> p z c").bitcast(I32))
        nc.sync.dma_start(out=xq[0][:].bitcast(I32), in_=xq_view[:, :, 0:HALF])
        nc.sync.dma_start(out=xq[1][:].bitcast(I32), in_=xq_view[:, :, HALF:T])
        nc.sync.dma_start(out=u_cols[:], in_=us.rearrange("(p j) o -> p (j o)", j=PACK))
        nc.sync.dma_start(out=wu[:].bitcast(I32), in_=wu_words[0].rearrange("p c r -> p (c r)").bitcast(I32))
        for q in range(4):
            load_scales(nc.sync, wu_plane, wu_scales, q)

        warm = ps.tile([P, T], F32, name="y_bank", tag="early0")

        def warm_pass():
            nc.tensor.matmul_mx(
                out=warm[:],
                lhsT=zero_codes[:].bitcast(E4M3),
                lhsT_scale=zero_plane[:],
                rhs=dc_codes[:, 0:T].bitcast(E5M2),
                rhs_scale=dc_plane[:, 0:T],
                start=True,
                stop=True,
            )

        for i in range(WARM_PASSES):
            warm_pass()

        d_bank = [ps.tile([P, R], F32, name="d_bank%d" % c) for c in range(CHUNKS)]

        def interleave_g(c):
            copy = nc.vector.tensor_copy if c < 2 else nc.scalar.copy
            copy(
                out=g_bf[c][:].rearrange("p (c i j) -> p c j i", i=4, j=PACK),
                in_=g_src[c].rearrange("p j (c i) -> p c j i", i=4),
            )

        def quantize_g(c):
            nc.vector.quantize_mx(out=g_codes[c][:].bitcast(E5M2), scales=g_plane[c][:], in_=g_bf[c][:])

        def x_pass(c, z):
            lo = (c % 2) * TC
            nc.tensor.matmul_mx(
                out=d_bank[c][:],
                lhsT=xq[c // 2][:, z, lo : lo + TC].bitcast(E4M3),
                lhsT_scale=planes[:, (XQ + z) * 512 + c * TC : (XQ + z) * 512 + (c + 1) * TC],
                rhs=ws[:, z, :].bitcast(E2M1),
                rhs_scale=planes[:, (WS + z) * 512 : (WS + z + 1) * 512],
                start=False,
                stop=(z == 1),
            )

        def g_pass(c):
            nc.tensor.matmul_mx(
                out=d_bank[c][:],
                lhsT=g_codes[c][:].bitcast(E5M2),
                lhsT_scale=g_plane[c][:],
                rhs=wd[:].bitcast(E2M1),
                rhs_scale=planes[:, WD * 512 : (WD + 1) * 512],
                start=True,
                stop=False,
            )

        def clip(c):
            for j in (0, 2):
                nc.vector.tensor_scalar(
                    out=clipped[c][:, j : j + 2, :],
                    in0=d_bank[c][:].rearrange("t (p j) -> t j p", j=PACK)[:, j : j + 2, :],
                    scalar1=1.0,
                    scalar2=-1.0,
                    op0=ALU.min,
                    op1=ALU.max,
                )

        turned = {}

        def turn(c, tag):
            bank = ps.tile([P, PACK, TC], F32, name="turned", tag=tag)
            turned[c] = bank
            for j in range(PACK):
                nc.tensor.transpose(bank[:, j, :], clipped[c][:, j, :], ident[:])

        def scale(c):
            nc.vector.tensor_tensor(
                out=dc_bf[c][:].rearrange("p (t j) -> p t j", j=PACK),
                in0=turned[c][:].rearrange("p j t -> p t j"),
                in1=u_cols[:].unsqueeze(1).to_broadcast([P, TC, PACK]),
                op=ALU.mult,
            )

        def quantize_dc(c):
            cols = slice(T + c * TC, T + (c + 1) * TC)
            nc.vector.quantize_mx(out=dc_codes[:, cols].bitcast(E5M2), scales=dc_plane[:, cols], in_=dc_bf[c][:])

        y_bank = {}

        def y_pass(h, m, tag):
            bank = ps.tile([P, T], F32, name="y_bank", tag=tag)
            y_bank[h, m] = bank
            cols = slice((h + 1) * HALF, (h + 1) * HALF + T)
            nc.tensor.matmul_mx(
                out=bank[:],
                lhsT=wu[:, m * P : (m + 1) * P].bitcast(E4M3),
                lhsT_scale=wu_plane[:, 0, m * P : (m + 1) * P],
                rhs=dc_codes[:, cols].bitcast(E5M2),
                rhs_scale=dc_plane[:, cols],
                start=True,
                stop=True,
            )

        def y_out(h, m, on_vector):
            if on_vector:
                nc.vector.tensor_copy(out=res[h][m][:], in_=y_bank[h, m][:, HALF:T])
            else:
                nc.scalar.copy(out=res[h][m][:], in_=y_bank[h, m][:, HALF:T])
            nc.sync.dma_start(out=out[m * P : (m + 1) * P, h * HALF : (h + 1) * HALF], in_=res[h][m][:])

        for c in range(CHUNKS):
            interleave_g(c)
        for c in range(CHUNKS):
            quantize_g(c)
        for c in range(3):
            g_pass(c)
        for c in range(3):
            x_pass(c, 0)
            x_pass(c, 1)
            clip(c)
        turn(0, "turned0")
        turn(1, "turned1")
        g_pass(3)
        x_pass(3, 0)
        x_pass(3, 1)
        turn(2, "d_bank0")
        warm_pass()
        scale(0)
        scale(1)
        clip(3)
        turn(3, "d_bank1")
        quantize_dc(0)
        quantize_dc(1)
        for m, tag in enumerate(("early0", "early1", "turned0", "turned1")):
            y_pass(0, m, tag)
            y_out(0, m, False)
        scale(2)
        scale(3)
        quantize_dc(2)
        quantize_dc(3)
        for m, tag in enumerate(("d_bank2", "d_bank3", "d_bank0", "d_bank1")):
            y_pass(1, m, tag)
        for m in range(4):
            y_out(1, m, m % 2 == 0)
